import numpy as np
import ml_dtypes


def mxq(x, axis, fmt="e4m3"):
    dtype, down = {"e4m3": (ml_dtypes.float8_e4m3fn, 7), "e5m2": (ml_dtypes.float8_e5m2, 14)}[fmt]
    v = np.moveaxis(np.asarray(x, np.float32).astype(ml_dtypes.bfloat16).astype(np.float64), axis, -1)
    blocks = v.reshape(v.shape[:-1] + (-1, 32))
    amax = np.abs(blocks).max(-1, keepdims=True)
    byte = np.maximum(np.where(amax > 0, np.frexp(amax)[1] - 1 + 127, 0) - down, 1)
    scale = np.exp2(byte - 127.0)
    codes = (blocks / scale).astype(np.float32).astype(dtype).astype(np.float64)
    return np.moveaxis((codes * scale).reshape(v.shape), -1, axis)


WIDE = False


def mx_kscale(k):
    if not WIDE:
        return np.ones(k)
    levels = np.array([10, -10, 5, -5, 0])
    if k % 512:
        return np.exp2(np.random.permutation(np.resize(levels, k // 32))).repeat(32)
    a = np.empty((k // 512, 16))
    for p in range(k // 512):
        a[p, :8] = np.random.permutation(np.resize(levels, 8))
        for g in range(8):
            far = levels[np.abs(levels - a[p, g]) >= 10]
            a[p, g + 8] = far[np.random.randint(len(far))]
    return np.exp2(a.ravel()).repeat(32)


def f64(x):
    return np.asarray(x).astype(np.float64)


def striped(idx):
    return np.tile(idx.reshape(-1, 16).T, (8, 1)).astype(np.uint16)


def unstriped(offs):
    return offs[:16].T.reshape(-1).astype(np.int64)


E2M1 = np.array([0.0, 0.5, 1.0, 1.5, 2.0, 3.0, 4.0, 6.0, -0.0, -0.5, -1.0, -1.5, -2.0, -3.0, -4.0, -6.0])


def pack_weight(w, fmt):
    k, n = w.shape
    w = f64(np.asarray(w, np.float32).astype(ml_dtypes.bfloat16)).reshape(k // 32, 32, n)
    amax = np.abs(w).max(1)
    if fmt == "e4m3":
        byte = np.frexp(amax)[1] - 1 + 127 - 7
    else:
        mant, ex = np.frexp(amax / 6.0)
        byte = np.where(mant > 0.5, ex, ex - 1) + 127
    byte = np.clip(np.where(amax > 0, byte, 1), 1, 254)
    scaled = (w * np.exp2(127.0 - byte)[:, None, :]).reshape(k, n).astype(np.float32)
    by_word = np.ascontiguousarray(scaled.reshape(k // 512, 128, 4, n).transpose(0, 1, 3, 2))
    if fmt == "e4m3":
        words = by_word.astype(ml_dtypes.float8_e4m3fn).view(np.uint8)
    else:
        c = by_word.astype(ml_dtypes.float4_e2m1fn).view(np.uint8) & 0xF
        words = (c[..., 0::2] | (c[..., 1::2] << 4)).reshape(k // 512, 128, 2 * n)
    return np.ascontiguousarray(words), np.ascontiguousarray(byte.astype(np.uint8).reshape(k // 512, 16, n))


def unpack_weight(words, scales, fmt):
    g, _, n = scales.shape
    words = np.ascontiguousarray(words).reshape(g, 128, n, -1)
    if fmt == "e4m3":
        vals = words.view(ml_dtypes.float8_e4m3fn).astype(np.float64)
    else:
        nib = np.empty((g, 128, n, 4), np.uint8)
        nib[..., 0::2] = words & 0xF
        nib[..., 1::2] = words >> 4
        vals = E2M1[nib]
    vals = vals * np.repeat(np.exp2(scales.astype(np.float64) - 127.0), 8, axis=1)[..., None]
    return vals.transpose(0, 1, 3, 2).reshape(g * 512, n)


K, T, E, C, N = 1536, 640, 4, 128, 512
K8 = 512


def by_expert(wq, xq):
    return np.concatenate([wq[e].T @ xq[:, e * C:(e + 1) * C] for e in range(E)], axis=1)


def setup_inputs():
    n = np.random.standard_normal
    s = mx_kscale(K)[:, None]
    w = n((E, K, N)) / np.sqrt(K) / s[None]
    w8 = [pack_weight(m[:K8], "e4m3") for m in w]
    w4 = [pack_weight(m[K8:], "e2m1") for m in w]
    return {
        "xT": (n((K, T)) * s).astype(np.float32),
        "xr": n((N, T)).astype(np.float32),
        "w8_words": np.stack([m[0] for m in w8]),
        "w8_scales": np.stack([m[1] for m in w8]),
        "w4_words": np.stack([m[0] for m in w4]),
        "w4_scales": np.stack([m[1] for m in w4]),
        "gate": np.tile(np.random.uniform(0.2, 1.0, E * C), (N, 1)).astype(np.float32),
        "offs": striped(np.random.permutation(T)[:E * C]),
    }


def reference(xT, xr, w8_words, w8_scales, w4_words, w4_scales, gate, offs):
    idx = unstriped(offs)
    w = np.stack([np.concatenate([unpack_weight(w8_words[e], w8_scales[e], "e4m3"), unpack_weight(w4_words[e], w4_scales[e], "e2m1")]) for e in range(E)])
    xq = mxq(f64(xT)[:, idx], 0, "e4m3")
    y = by_expert(w, xq)
    out = f64(xr).copy()
    out[:, idx] += f64(gate) * y
    return out

@@ -1,0 +1,189 @@
+from contextlib import ExitStack
+
+import concourse.mybir as mybir
+from concourse.masks import make_identity
+
+K, T, E, C, N = 1536, 640, 4, 128, 512
+P = 128
+S = E * C
+PASSES = 3
+NB = N // P
+
+F32 = mybir.dt.float32
+BF16 = mybir.dt.bfloat16
+I32 = mybir.dt.int32
+U32 = mybir.dt.uint32
+U16 = mybir.dt.uint16
+U8 = mybir.dt.uint8
+FP8X4 = mybir.dt.float8_e4m3fn_x4
+FP4X4 = mybir.dt.float4_e2m1fn_x4
+COPY = mybir.ActivationFunctionType.Copy
+ADD = mybir.AluOpType.add
+
+FLOPS = 2 * K * N * S
+BYTES = 4 * K * T + 2 * 4 * N * T + E * 512 * N * 4 + E * 1024 * N // 2 + E * 48 * N + 4 * S + 2 * 128 * S // 16
+
+LOADS = (
+    (((0, 256), ((0, 256, "v"),)), ((256, 384), ((256, 256, "s"), (512, 128, "v")))),
+    (((0, 384), ((0, 256, "s"), (256, 128, "v"))), ((384, 256), ((384, 256, "s"),))),
+    (((0, 384), ((0, 256, "s"), (256, 128, "v"))), ((384, 256), ((384, 128, "s"), (512, 128, "v")))),
+)
+
+
+def tile_moe_res_lin_none_kernel(tc, xT, xr, w8_words, w8_scales, w4_words, w4_scales, gate, offs, out):
+    nc = tc.nc
+    with ExitStack() as ctx:
+        keep = ctx.enter_context(tc.tile_pool(name="keep", bufs=1))
+        psum = ctx.enter_context(tc.psum_pool(name="psum", bufs=1))
+
+        offsets = keep.tile([P, S // 16], U16, name="offsets")
+        w8 = keep.tile([P, E, 4 * N], U8, name="w8", align_bytes=64)
+        w4 = keep.tile([P, 2 * E, 2 * N], U8, name="w4", align_bytes=64)
+        w8s = keep.tile([P, E, N], U8, name="w8s", align_bytes=64)
+        w4s = keep.tile([P, 2 * E, N], U8, name="w4s", align_bytes=64)
+        residual = keep.tile([P, NB, T], F32, name="residual")
+        gate_rows = keep.tile([P, P], F32, name="gate_rows")
+        gate_cols = keep.tile([P, E], F32, name="gate_cols")
+        ident = keep.tile([P, P], F32, name="ident")
+        windows = [keep.tile([P, T], F32, name=f"window{b}") for b in range(NB)]
+        results = [keep.tile([P, T], F32, name=f"result{b}") for b in range(NB)]
+        words = [keep.tile([P, T], U32, name=f"words{a}", align_bytes=64) for a in range(PASSES)]
+        scales = [keep.tile([P, T], U8, name=f"scales{a}", align_bytes=64) for a in range(PASSES)]
+        slot_words = [keep.tile([P, S], U32, name=f"slot_words{a}", align_bytes=64) for a in range(PASSES)]
+        slot_scales = [keep.tile([P, S], U8, name=f"slot_scales{a}", align_bytes=64) for a in range(PASSES)]
+        slot_y = keep.tile([P, NB, S], F32, name="slot_y")
+        warm = keep.tile([P, 1], F32, name="warm")
+
+        nc.vector.memset(warm[:], 0.0)
+        nc.scalar.copy(warm[:], warm[:])
+        for a in range(PASSES):
+            nc.gpsimd.memset(scales[a][:], 0)
+        nc.gpsimd.memset(gate_rows[:], 0.0)
+        make_identity(nc, ident[:])
+        nc.vector.memset(w8s[:].rearrange("p e n -> p (e n)").bitcast(I32), 0)
+        nc.vector.memset(w4s[:].rearrange("p e n -> p (e n)").bitcast(I32), 0)
+
+        x_src = xT.rearrange("(a p j) t -> a p j t", a=PASSES, j=4)
+        raw = {}
+        for a in range(PASSES):
+            for i, ((t0, width), pieces) in enumerate(LOADS[a]):
+                tile = keep.tile([P, 4, width], F32, name=f"raw{a}_{i}")
+                nc.sync.dma_start(tile[:], x_src[a, :, :, t0 : t0 + width])
+                raw[a, i] = tile
+                if a == 0 and i == 0:
+                    nc.sync.dma_start(offsets[:], offs)
+                    nc.sync.dma_start(gate_rows[0:E, :], gate[0:1, :].rearrange("o (e c) -> (o e) c", c=C))
+        for src, dst in ((w8_scales, w8s), (w4_scales, w4s)):
+            rows = src.rearrange("e a q n -> q (e a) n").bitcast(I32)
+            for q in range(4):
+                nc.sync.dma_start(dst[32 * q : 32 * q + 4, :, :].bitcast(I32), rows[4 * q : 4 * q + 4])
+        w8_src = w8_words.rearrange("e a p n r -> p (e a) (n r)").bitcast(I32)
+        w4_src = w4_words.rearrange("e a p b -> p (e a) b").bitcast(I32)
+        for h in range(2):
+            nc.sync.dma_start(w8[:, 2 * h : 2 * h + 2, :].bitcast(I32), w8_src[:, 2 * h : 2 * h + 2, :])
+            nc.sync.dma_start(w4[:, 4 * h : 4 * h + 4, :].bitcast(I32), w4_src[:, 4 * h : 4 * h + 4, :])
+        xr_src = xr.rearrange("(b p) t -> p b t", p=P)
+        for h in range(2):
+            nc.sync.dma_start(residual[:, 2 * h : 2 * h + 2, :], xr_src[:, 2 * h : 2 * h + 2, :])
+
+        turned_gate = psum.tile([P, NB, P], F32, name="turned_gate", tag="turned", bufs=4)
+        nc.tensor.transpose(turned_gate[:, 0, :], gate_rows[:], ident[:])
+        nc.scalar.copy(gate_cols[:], turned_gate[:, 0, 0:E])
+
+        def cast(a):
+            done = []
+            for i, ((t0, width), pieces) in enumerate(LOADS[a]):
+                for u0, n, engine in pieces:
+                    grouped = keep.tile([P, n, 4], BF16, name=f"grouped{a}_{u0}", align_bytes=64)
+                    src = raw[a, i][:, :, u0 - t0 : u0 - t0 + n].rearrange("p j t -> p t j")
+                    if engine == "v":
+                        nc.vector.tensor_copy(grouped[:], src)
+                    else:
+                        nc.scalar.copy(grouped[:], src)
+                    done.append((u0, n, grouped))
+            return done
+
+        def quantise_pass(a):
+            for u0, n, grouped in cast(a):
+                nc.vector.quantize_mx(
+                    out=words[a][:, u0 : u0 + n].bitcast(FP8X4),
+                    scales=scales[a][:, u0 : u0 + n],
+                    in_=grouped[:].rearrange("p t j -> p (t j)"),
+                )
+
+        def gather(a, h):
+            cols = slice(h * S // 2, (h + 1) * S // 2)
+            part = offsets[:, h * S // 32 : (h + 1) * S // 32]
+            nc.vector.tensor_copy(slot_words[a][:, cols], words[a][:].indirect(part))
+            nc.vector.tensor_copy(slot_scales[a][:, cols], scales[a][:].indirect(part))
+
+        banks = [psum.tile([P, N], F32, name=f"bank{e}") for e in range(E)]
+
+        def multiply(a, e):
+            cols = slice(e * C, (e + 1) * C)
+            if a == 0:
+                rhs, rhs_scale = w8[:, e, :].bitcast(FP8X4), w8s[:, e, :]
+            else:
+                rhs, rhs_scale = w4[:, 2 * e + a - 1, :].bitcast(FP4X4), w4s[:, 2 * e + a - 1, :]
+            nc.tensor.matmul_mx(
+                out=banks[e][:],
+                lhsT=slot_words[a][:, cols].bitcast(FP8X4),
+                lhsT_scale=slot_scales[a][:, cols],
+                rhs=rhs,
+                rhs_scale=rhs_scale,
+                start=(a == 0),
+                stop=(a == PASSES - 1),
+            )
+
+        def turn(e):
+            gated = keep.tile([P, N], F32, name=f"gated{e}")
+            nc.scalar.activation(gated[:], banks[e][:], COPY, scale=gate_cols[:, e : e + 1])
+            turned = psum.tile([P, NB, P], F32, name=f"turned{e}", tag="turned", bufs=4)
+            for b in range(NB):
+                nc.tensor.transpose(turned[:, b, :], gated[:, b * P : (b + 1) * P], ident[:])
+            nc.scalar.copy(slot_y[:, :, e * C : (e + 1) * C], turned[:])
+
+        def scatter(b, h):
+            cols = slice(h * S // 2, (h + 1) * S // 2)
+            part = offsets[:, h * S // 32 : (h + 1) * S // 32]
+            nc.vector.tensor_copy(windows[b][:].indirect(part), slot_y[:, b, cols])
+
+        def finish(b, engine):
+            engine.tensor_tensor(results[b][:], windows[b][:], residual[:, b, :], ADD)
+            nc.sync.dma_start(out[b * P : (b + 1) * P, :], results[b][:])
+
+        for b in range(NB):
+            nc.gpsimd.memset(windows[b][:], 0.0)
+
+        quantise_pass(0)
+        gather(0, 0)
+        gather(0, 1)
+        quantise_pass(1)
+        gather(1, 0)
+        quantise_pass(2)
+        gather(2, 0)
+        for e in (0, 1):
+            for a in range(PASSES):
+                multiply(a, e)
+        gather(1, 1)
+        for e in (0, 1):
+            turn(e)
+        gather(2, 1)
+        for e in (2, 3):
+            for a in range(PASSES):
+                multiply(a, e)
+        for e in (2, 3):
+            turn(e)
+
+        scatter(0, 0)
+        scatter(1, 0)
+        scatter(0, 1)
+        finish(0, nc.gpsimd)
+        scatter(1, 1)
+        finish(1, nc.gpsimd)
+        scatter(2, 0)
+        scatter(2, 1)
+        finish(2, nc.gpsimd)
+        scatter(3, 0)
+        scatter(3, 1)
+        finish(3, nc.vector)

@@ -25,8 +25,8 @@ BYTES = 4 * K * T + 2 * 4 * N * T + E * 512 * N * 4 + E * 1024 * N // 2 + E * 48
 
 LOADS = (
     (((0, 256), ((0, 256, "v"),)), ((256, 384), ((256, 256, "s"), (512, 128, "v")))),
-    (((0, 384), ((0, 256, "s"), (256, 128, "v"))), ((384, 256), ((384, 256, "s"),))),
-    (((0, 384), ((0, 256, "s"), (256, 128, "v"))), ((384, 256), ((384, 128, "s"), (512, 128, "v")))),
+    (((0, 640), ((0, 256, "s"), (256, 128, "v"), (384, 256, "s"))),),
+    (((0, 640), ((0, 256, "s"), (256, 256, "v"), (512, 128, "v"))),),
 )
 
 
@@ -48,35 +48,46 @@ def tile_moe_res_lin_none_kernel(tc, xT, xr, w8_words, w8_scales, w4_words, w4_s
         windows = [keep.tile([P, T], F32, name=f"window{b}") for b in range(NB)]
         results = [keep.tile([P, T], F32, name=f"result{b}") for b in range(NB)]
         words = [keep.tile([P, T], U32, name=f"words{a}", align_bytes=64) for a in range(PASSES)]
-        scales = [keep.tile([P, T], U8, name=f"scales{a}", align_bytes=64) for a in range(PASSES)]
+        scales = [keep.tile([P, T], U8, name=f"scales{a}", align_bytes=64) for a in range(2)]
         slot_words = [keep.tile([P, S], U32, name=f"slot_words{a}", align_bytes=64) for a in range(PASSES)]
-        slot_scales = [keep.tile([P, S], U8, name=f"slot_scales{a}", align_bytes=64) for a in range(PASSES)]
+        slot_scales = [keep.tile([P, S], U8, name=f"slot_scales{a}", align_bytes=64) for a in range(2)]
+        planes = ((0, 4), (0, 0), (1, 0))
         slot_y = keep.tile([P, NB, S], F32, name="slot_y")
         warm = keep.tile([P, 1], F32, name="warm")
 
         nc.vector.memset(warm[:], 0.0)
         nc.scalar.copy(warm[:], warm[:])
-        for a in range(PASSES):
-            nc.gpsimd.memset(scales[a][:], 0)
+        for plane in scales:
+            nc.gpsimd.memset(plane[:].bitcast(I32), 0)
         nc.gpsimd.memset(gate_rows[:], 0.0)
         make_identity(nc, ident[:])
         nc.vector.memset(w8s[:].rearrange("p e n -> p (e n)").bitcast(I32), 0)
         nc.vector.memset(w4s[:].rearrange("p e n -> p (e n)").bitcast(I32), 0)
+        for b in range(NB):
+            nc.vector.memset(windows[b][:], 0.0)
 
         x_src = xT.rearrange("(a p j) t -> a p j t", a=PASSES, j=4)
         raw = {}
-        for a in range(PASSES):
-            for i, ((t0, width), pieces) in enumerate(LOADS[a]):
-                tile = keep.tile([P, 4, width], F32, name=f"raw{a}_{i}")
-                nc.sync.dma_start(tile[:], x_src[a, :, :, t0 : t0 + width])
-                raw[a, i] = tile
-                if a == 0 and i == 0:
-                    nc.sync.dma_start(offsets[:], offs)
-                    nc.sync.dma_start(gate_rows[0:E, :], gate[0:1, :].rearrange("o (e c) -> (o e) c", c=C))
-        for src, dst in ((w8_scales, w8s), (w4_scales, w4s)):
+
+        def load_tokens(a, i):
+            t0, width = LOADS[a][i][0]
+            tile = keep.tile([P, 4, width], F32, name=f"raw{a}_{i}")
+            nc.sync.dma_start(tile[:], x_src[a, :, :, t0 : t0 + width])
+            raw[a, i] = tile
+
+        def load_scales(src, dst):
             rows = src.rearrange("e a q n -> q (e a) n").bitcast(I32)
             for q in range(4):
                 nc.sync.dma_start(dst[32 * q : 32 * q + 4, :, :].bitcast(I32), rows[4 * q : 4 * q + 4])
+
+        load_tokens(0, 0)
+        nc.sync.dma_start(offsets[:], offs)
+        load_tokens(0, 1)
+        load_scales(w8_scales, w8s)
+        load_tokens(1, 0)
+        nc.sync.dma_start(gate_rows[0:E, :], gate[0:1, :].rearrange("o (e c) -> (o e) c", c=C))
+        load_scales(w4_scales, w4s)
+        load_tokens(2, 0)
         w8_src = w8_words.rearrange("e a p n r -> p (e a) (n r)").bitcast(I32)
         w4_src = w4_words.rearrange("e a p b -> p (e a) b").bitcast(I32)
         for h in range(2):
@@ -104,18 +115,24 @@ def tile_moe_res_lin_none_kernel(tc, xT, xr, w8_words, w8_scales, w4_words, w4_s
             return done
 
         def quantise_pass(a):
+            plane, row = planes[a]
             for u0, n, grouped in cast(a):
                 nc.vector.quantize_mx(
                     out=words[a][:, u0 : u0 + n].bitcast(FP8X4),
-                    scales=scales[a][:, u0 : u0 + n],
+                    scales=scales[plane][row:P, u0 : u0 + n],
                     in_=grouped[:].rearrange("p t j -> p (t j)"),
                 )
 
-        def gather(a, h):
+        def gather(table, slots, h):
             cols = slice(h * S // 2, (h + 1) * S // 2)
             part = offsets[:, h * S // 32 : (h + 1) * S // 32]
-            nc.vector.tensor_copy(slot_words[a][:, cols], words[a][:].indirect(part))
-            nc.vector.tensor_copy(slot_scales[a][:, cols], scales[a][:].indirect(part))
+            nc.vector.tensor_copy(slots[:, cols], table[:].indirect(part))
+
+        def gather_words(a, h):
+            gather(words[a], slot_words[a], h)
+
+        def gather_scales(i, h):
+            gather(scales[i], slot_scales[i], h)
 
         banks = [psum.tile([P, N], F32, name=f"bank{e}") for e in range(E)]
 
@@ -128,7 +145,7 @@ def tile_moe_res_lin_none_kernel(tc, xT, xr, w8_words, w8_scales, w4_words, w4_s
             nc.tensor.matmul_mx(
                 out=banks[e][:],
                 lhsT=slot_words[a][:, cols].bitcast(FP8X4),
-                lhsT_scale=slot_scales[a][:, cols],
+                lhsT_scale=slot_scales[planes[a][0]][planes[a][1] : P, cols],
                 rhs=rhs,
                 rhs_scale=rhs_scale,
                 start=(a == 0),
@@ -152,23 +169,24 @@ def tile_moe_res_lin_none_kernel(tc, xT, xr, w8_words, w8_scales, w4_words, w4_s
             engine.tensor_tensor(results[b][:], windows[b][:], residual[:, b, :], ADD)
             nc.sync.dma_start(out[b * P : (b + 1) * P, :], results[b][:])
 
-        for b in range(NB):
-            nc.gpsimd.memset(windows[b][:], 0.0)
-
         quantise_pass(0)
-        gather(0, 0)
-        gather(0, 1)
+        gather_words(0, 0)
+        gather_words(0, 1)
         quantise_pass(1)
-        gather(1, 0)
+        gather_words(1, 0)
+        gather_scales(0, 0)
         quantise_pass(2)
-        gather(2, 0)
+        gather_words(2, 0)
+        gather_scales(1, 0)
         for e in (0, 1):
             for a in range(PASSES):
                 multiply(a, e)
-        gather(1, 1)
+        gather_words(1, 1)
+        gather_scales(0, 1)
         for e in (0, 1):
             turn(e)
-        gather(2, 1)
+        gather_words(2, 1)
+        gather_scales(1, 1)
         for e in (2, 3):
             for a in range(PASSES):
                 multiply(a, e)

@@ -8,6 +8,7 @@ P = 128
 S = E * C
 PASSES = 3
 NB = N // P
+WIDE = 704
 
 F32 = mybir.dt.float32
 BF16 = mybir.dt.bfloat16
@@ -24,9 +25,9 @@ FLOPS = 2 * K * N * S
 BYTES = 4 * K * T + 2 * 4 * N * T + E * 512 * N * 4 + E * 1024 * N // 2 + E * 48 * N + 4 * S + 2 * 128 * S // 16
 
 LOADS = (
-    (((0, 256), ((0, 256, "v"),)), ((256, 384), ((256, 256, "s"), (512, 128, "v")))),
-    (((0, 640), ((0, 256, "s"), (256, 128, "v"), (384, 256, "s"))),),
-    (((0, 640), ((0, 256, "s"), (256, 256, "v"), (512, 128, "v"))),),
+    ((0, 256, ((256, "v"),), (256,)), (256, 384, ((256, "v"), (128, "s")), (256, 128))),
+    ((0, 384, ((256, "s"), (128, "v")), (256, 128)), (384, 256, ((128, "s"), (128, "v")), (256,))),
+    ((0, 256, ((256, "s"),), (256,)), (256, 256, ((192, "v"), (64, "s")), (256,)), (512, 128, ((128, "s"),), (128,))),
 )
 
 
@@ -45,14 +46,14 @@ def tile_moe_res_lin_none_kernel(tc, xT, xr, w8_words, w8_scales, w4_words, w4_s
         gate_rows = keep.tile([P, P], F32, name="gate_rows")
         gate_cols = keep.tile([P, E], F32, name="gate_cols")
         ident = keep.tile([P, P], F32, name="ident")
-        windows = [keep.tile([P, T], F32, name=f"window{b}") for b in range(NB)]
+        windows = [keep.tile([P, T if b < 2 else WIDE], F32, name=f"window{b}") for b in range(NB)]
+        slot_y = [keep.tile([P, S], F32, name=f"slot_y{b}") for b in range(NB)]
         results = [keep.tile([P, T], F32, name=f"result{b}") for b in range(NB)]
         words = [keep.tile([P, T], U32, name=f"words{a}", align_bytes=64) for a in range(PASSES)]
         scales = [keep.tile([P, T], U8, name=f"scales{a}", align_bytes=64) for a in range(2)]
         slot_words = [keep.tile([P, S], U32, name=f"slot_words{a}", align_bytes=64) for a in range(PASSES)]
         slot_scales = [keep.tile([P, S], U8, name=f"slot_scales{a}", align_bytes=64) for a in range(2)]
         planes = ((0, 4), (0, 0), (1, 0))
-        slot_y = keep.tile([P, NB, S], F32, name="slot_y")
         warm = keep.tile([P, 1], F32, name="warm")
 
         nc.vector.memset(warm[:], 0.0)
@@ -64,13 +65,13 @@ def tile_moe_res_lin_none_kernel(tc, xT, xr, w8_words, w8_scales, w4_words, w4_s
         nc.vector.memset(w8s[:].rearrange("p e n -> p (e n)").bitcast(I32), 0)
         nc.vector.memset(w4s[:].rearrange("p e n -> p (e n)").bitcast(I32), 0)
         for b in range(NB):
-            nc.vector.memset(windows[b][:], 0.0)
+            nc.gpsimd.memset(windows[b][:], 0.0)
 
         x_src = xT.rearrange("(a p j) t -> a p j t", a=PASSES, j=4)
         raw = {}
 
         def load_tokens(a, i):
-            t0, width = LOADS[a][i][0]
+            t0, width, casts, pieces = LOADS[a][i]
             tile = keep.tile([P, 4, width], F32, name=f"raw{a}_{i}")
             nc.sync.dma_start(tile[:], x_src[a, :, :, t0 : t0 + width])
             raw[a, i] = tile
@@ -85,9 +86,12 @@ def tile_moe_res_lin_none_kernel(tc, xT, xr, w8_words, w8_scales, w4_words, w4_s
         load_tokens(0, 1)
         load_scales(w8_scales, w8s)
         load_tokens(1, 0)
+        load_tokens(1, 1)
         nc.sync.dma_start(gate_rows[0:E, :], gate[0:1, :].rearrange("o (e c) -> (o e) c", c=C))
         load_scales(w4_scales, w4s)
         load_tokens(2, 0)
+        load_tokens(2, 1)
+        load_tokens(2, 2)
         w8_src = w8_words.rearrange("e a p n r -> p (e a) (n r)").bitcast(I32)
         w4_src = w4_words.rearrange("e a p b -> p (e a) b").bitcast(I32)
         for h in range(2):
@@ -97,31 +101,35 @@ def tile_moe_res_lin_none_kernel(tc, xT, xr, w8_words, w8_scales, w4_words, w4_s
         for h in range(2):
             nc.sync.dma_start(residual[:, 2 * h : 2 * h + 2, :], xr_src[:, 2 * h : 2 * h + 2, :])
 
-        turned_gate = psum.tile([P, NB, P], F32, name="turned_gate", tag="turned", bufs=4)
-        nc.tensor.transpose(turned_gate[:, 0, :], gate_rows[:], ident[:])
+        turned_gate = psum.tile([P, 2, 2 * C], F32, name="turned_gate", tag="turned", bufs=4)
+        nc.tensor.transpose(turned_gate[:, 0, 0:P], gate_rows[:], ident[:])
         nc.scalar.copy(gate_cols[:], turned_gate[:, 0, 0:E])
-
-        def cast(a):
-            done = []
-            for i, ((t0, width), pieces) in enumerate(LOADS[a]):
-                for u0, n, engine in pieces:
-                    grouped = keep.tile([P, n, 4], BF16, name=f"grouped{a}_{u0}", align_bytes=64)
-                    src = raw[a, i][:, :, u0 - t0 : u0 - t0 + n].rearrange("p j t -> p t j")
-                    if engine == "v":
-                        nc.vector.tensor_copy(grouped[:], src)
-                    else:
-                        nc.scalar.copy(grouped[:], src)
-                    done.append((u0, n, grouped))
-            return done
 
         def quantise_pass(a):
             plane, row = planes[a]
-            for u0, n, grouped in cast(a):
-                nc.vector.quantize_mx(
-                    out=words[a][:, u0 : u0 + n].bitcast(FP8X4),
-                    scales=scales[plane][row:P, u0 : u0 + n],
-                    in_=grouped[:].rearrange("p t j -> p (t j)"),
-                )
+            staged = []
+            for i, (t0, width, casts, pieces) in enumerate(LOADS[a]):
+                grouped = keep.tile([P, width, 4], BF16, name=f"grouped{a}_{i}", align_bytes=64)
+                u0 = 0
+                for n, engine in casts:
+                    src = raw[a, i][:, :, u0 : u0 + n].rearrange("p j (c i) -> p c j i", i=4)
+                    dst = grouped[:, u0 : u0 + n, :].rearrange("p (c i) j -> p c j i", i=4)
+                    if engine == "v":
+                        nc.vector.tensor_copy(dst, src)
+                    else:
+                        nc.scalar.copy(dst, src)
+                    u0 += n
+                staged.append(grouped)
+            for grouped, (t0, width, casts, pieces) in zip(staged, LOADS[a]):
+                u0 = 0
+                for n in pieces:
+                    cols = slice(t0 + u0, t0 + u0 + n)
+                    nc.vector.quantize_mx(
+                        out=words[a][:, cols].bitcast(FP8X4),
+                        scales=scales[plane][row:P, cols],
+                        in_=grouped[:, u0 : u0 + n, :].rearrange("p t j -> p (t j)"),
+                    )
+                    u0 += n
 
         def gather(table, slots, h):
             cols = slice(h * S // 2, (h + 1) * S // 2)
@@ -152,22 +160,30 @@ def tile_moe_res_lin_none_kernel(tc, xT, xr, w8_words, w8_scales, w4_words, w4_s
                 stop=(a == PASSES - 1),
             )
 
-        def turn(e):
-            gated = keep.tile([P, N], F32, name=f"gated{e}")
-            nc.scalar.activation(gated[:], banks[e][:], COPY, scale=gate_cols[:, e : e + 1])
-            turned = psum.tile([P, NB, P], F32, name=f"turned{e}", tag="turned", bufs=4)
-            for b in range(NB):
-                nc.tensor.transpose(turned[:, b, :], gated[:, b * P : (b + 1) * P], ident[:])
-            nc.scalar.copy(slot_y[:, :, e * C : (e + 1) * C], turned[:])
+        def turn(h):
+            for half in range(2):
+                turned = psum.tile([P, 2, 2 * C], F32, name=f"turned{h}{half}", tag="turned", bufs=4)
+                for i in range(2):
+                    e = 2 * h + i
+                    gated = keep.tile([P, 2 * P], F32, name=f"gated{e}{half}")
+                    nc.scalar.activation(gated[:], banks[e][:, half * 2 * P : (half + 1) * 2 * P], COPY, scale=gate_cols[:, e : e + 1])
+                    for b in range(2):
+                        nc.tensor.transpose(turned[:, b, i * C : (i + 1) * C], gated[:, b * P : (b + 1) * P], ident[:])
+                for b in range(2):
+                    nc.scalar.copy(slot_y[2 * half + b][:, 2 * h * C : 2 * (h + 1) * C], turned[:, b, :])
 
         def scatter(b, h):
-            cols = slice(h * S // 2, (h + 1) * S // 2)
             part = offsets[:, h * S // 32 : (h + 1) * S // 32]
-            nc.vector.tensor_copy(windows[b][:].indirect(part), slot_y[:, b, cols])
+            nc.vector.tensor_copy(windows[b][:].indirect(part), slot_y[b][:, 2 * h * C : 2 * (h + 1) * C])
 
-        def finish(b, engine):
-            engine.tensor_tensor(results[b][:], windows[b][:], residual[:, b, :], ADD)
-            nc.sync.dma_start(out[b * P : (b + 1) * P, :], results[b][:])
+        def scatter_all(b):
+            nc.vector.tensor_copy(windows[b][:].indirect(offsets[:]), slot_y[b][:])
+
+        def finish(b, engine, parts):
+            for i in range(parts):
+                cols = slice(i * T // parts, (i + 1) * T // parts)
+                engine.tensor_tensor(results[b][:, cols], windows[b][:, cols], residual[:, b, cols], ADD)
+                nc.sync.dma_start(out[b * P : (b + 1) * P, cols], results[b][:, cols])
 
         quantise_pass(0)
         gather_words(0, 0)
@@ -183,25 +199,21 @@ def tile_moe_res_lin_none_kernel(tc, xT, xr, w8_words, w8_scales, w4_words, w4_s
                 multiply(a, e)
         gather_words(1, 1)
         gather_scales(0, 1)
-        for e in (0, 1):
-            turn(e)
+        turn(0)
         gather_words(2, 1)
         gather_scales(1, 1)
         for e in (2, 3):
             for a in range(PASSES):
                 multiply(a, e)
-        for e in (2, 3):
-            turn(e)
+        turn(1)
 
         scatter(0, 0)
         scatter(1, 0)
         scatter(0, 1)
-        finish(0, nc.gpsimd)
+        finish(0, nc.gpsimd, 1)
         scatter(1, 1)
-        finish(1, nc.gpsimd)
-        scatter(2, 0)
-        scatter(2, 1)
-        finish(2, nc.gpsimd)
-        scatter(3, 0)
-        scatter(3, 1)
-        finish(3, nc.vector)
+        finish(1, nc.gpsimd, 1)
+        scatter_all(2)
+        finish(2, nc.gpsimd, 1)
+        scatter_all(3)
+        finish(3, nc.vector, 2)

from contextlib import ExitStack

import concourse.mybir as mybir
from concourse.masks import make_identity

K, T, E, C, N = 1536, 640, 4, 128, 512
P = 128
S = E * C
PASSES = 3
NB = N // P
WIDE = 704

F32 = mybir.dt.float32
BF16 = mybir.dt.bfloat16
I32 = mybir.dt.int32
U32 = mybir.dt.uint32
U16 = mybir.dt.uint16
U8 = mybir.dt.uint8
FP8X4 = mybir.dt.float8_e4m3fn_x4
FP4X4 = mybir.dt.float4_e2m1fn_x4
COPY = mybir.ActivationFunctionType.Copy
ADD = mybir.AluOpType.add

FLOPS = 2 * K * N * S
BYTES = 4 * K * T + 2 * 4 * N * T + E * 512 * N * 4 + E * 1024 * N // 2 + E * 48 * N + 4 * S + 2 * 128 * S // 16

LOADS = (
    ((0, 256, ((256, "v"),), (256,)), (256, 384, ((256, "v"), (128, "s")), (256, 128))),
    ((0, 384, ((256, "s"), (128, "v")), (256, 128)), (384, 256, ((128, "s"), (128, "v")), (256,))),
    ((0, 256, ((256, "s"),), (256,)), (256, 256, ((192, "v"), (64, "s")), (256,)), (512, 128, ((128, "s"),), (128,))),
)


def tile_moe_res_lin_none_kernel(tc, xT, xr, w8_words, w8_scales, w4_words, w4_scales, gate, offs, out):
    nc = tc.nc
    with ExitStack() as ctx:
        keep = ctx.enter_context(tc.tile_pool(name="keep", bufs=1))
        psum = ctx.enter_context(tc.psum_pool(name="psum", bufs=1))

        offsets = keep.tile([P, S // 16], U16, name="offsets")
        w8 = keep.tile([P, E, 4 * N], U8, name="w8", align_bytes=64)
        w4 = keep.tile([P, 2 * E, 2 * N], U8, name="w4", align_bytes=64)
        w8s = keep.tile([P, E, N], U8, name="w8s", align_bytes=64)
        w4s = keep.tile([P, 2 * E, N], U8, name="w4s", align_bytes=64)
        residual = keep.tile([P, NB, T], F32, name="residual")
        gate_rows = keep.tile([P, P], F32, name="gate_rows")
        gate_cols = keep.tile([P, E], F32, name="gate_cols")
        ident = keep.tile([P, P], F32, name="ident")
        windows = [keep.tile([P, T if b < 2 else WIDE], F32, name=f"window{b}") for b in range(NB)]
        slot_y = [keep.tile([P, S], F32, name=f"slot_y{b}") for b in range(NB)]
        results = [keep.tile([P, T], F32, name=f"result{b}") for b in range(NB)]
        words = [keep.tile([P, T], U32, name=f"words{a}", align_bytes=64) for a in range(PASSES)]
        scales = [keep.tile([P, T], U8, name=f"scales{a}", align_bytes=64) for a in range(2)]
        slot_words = [keep.tile([P, S], U32, name=f"slot_words{a}", align_bytes=64) for a in range(PASSES)]
        slot_scales = [keep.tile([P, S], U8, name=f"slot_scales{a}", align_bytes=64) for a in range(2)]
        planes = ((0, 4), (0, 0), (1, 0))
        warm = keep.tile([P, 1], F32, name="warm")

        nc.vector.memset(warm[:], 0.0)
        nc.scalar.copy(warm[:], warm[:])
        for plane in scales:
            nc.gpsimd.memset(plane[:].bitcast(I32), 0)
        nc.gpsimd.memset(gate_rows[:], 0.0)
        make_identity(nc, ident[:])
        nc.vector.memset(w8s[:].rearrange("p e n -> p (e n)").bitcast(I32), 0)
        nc.vector.memset(w4s[:].rearrange("p e n -> p (e n)").bitcast(I32), 0)
        for b in range(NB):
            nc.gpsimd.memset(windows[b][:], 0.0)

        x_src = xT.rearrange("(a p j) t -> a p j t", a=PASSES, j=4)
        raw = {}

        def load_tokens(a, i):
            t0, width, casts, pieces = LOADS[a][i]
            tile = keep.tile([P, 4, width], F32, name=f"raw{a}_{i}")
            nc.sync.dma_start(tile[:], x_src[a, :, :, t0 : t0 + width])
            raw[a, i] = tile

        def load_scales(src, dst):
            rows = src.rearrange("e a q n -> q (e a) n").bitcast(I32)
            for q in range(4):
                nc.sync.dma_start(dst[32 * q : 32 * q + 4, :, :].bitcast(I32), rows[4 * q : 4 * q + 4])

        load_tokens(0, 0)
        nc.sync.dma_start(offsets[:], offs)
        load_tokens(0, 1)
        load_scales(w8_scales, w8s)
        load_tokens(1, 0)
        load_tokens(1, 1)
        nc.sync.dma_start(gate_rows[0:E, :], gate[0:1, :].rearrange("o (e c) -> (o e) c", c=C))
        load_scales(w4_scales, w4s)
        load_tokens(2, 0)
        load_tokens(2, 1)
        load_tokens(2, 2)
        w8_src = w8_words.rearrange("e a p n r -> p (e a) (n r)").bitcast(I32)
        w4_src = w4_words.rearrange("e a p b -> p (e a) b").bitcast(I32)
        for h in range(2):
            nc.sync.dma_start(w8[:, 2 * h : 2 * h + 2, :].bitcast(I32), w8_src[:, 2 * h : 2 * h + 2, :])
            nc.sync.dma_start(w4[:, 4 * h : 4 * h + 4, :].bitcast(I32), w4_src[:, 4 * h : 4 * h + 4, :])
        xr_src = xr.rearrange("(b p) t -> p b t", p=P)
        for h in range(2):
            nc.sync.dma_start(residual[:, 2 * h : 2 * h + 2, :], xr_src[:, 2 * h : 2 * h + 2, :])

        turned_gate = psum.tile([P, 2, 2 * C], F32, name="turned_gate", tag="turned", bufs=4)
        nc.tensor.transpose(turned_gate[:, 0, 0:P], gate_rows[:], ident[:])
        nc.scalar.copy(gate_cols[:], turned_gate[:, 0, 0:E])

        def quantise_pass(a):
            plane, row = planes[a]
            staged = []
            for i, (t0, width, casts, pieces) in enumerate(LOADS[a]):
                grouped = keep.tile([P, width, 4], BF16, name=f"grouped{a}_{i}", align_bytes=64)
                u0 = 0
                for n, engine in casts:
                    src = raw[a, i][:, :, u0 : u0 + n].rearrange("p j (c i) -> p c j i", i=4)
                    dst = grouped[:, u0 : u0 + n, :].rearrange("p (c i) j -> p c j i", i=4)
                    if engine == "v":
                        nc.vector.tensor_copy(dst, src)
                    else:
                        nc.scalar.copy(dst, src)
                    u0 += n
                staged.append(grouped)
            for grouped, (t0, width, casts, pieces) in zip(staged, LOADS[a]):
                u0 = 0
                for n in pieces:
                    cols = slice(t0 + u0, t0 + u0 + n)
                    nc.vector.quantize_mx(
                        out=words[a][:, cols].bitcast(FP8X4),
                        scales=scales[plane][row:P, cols],
                        in_=grouped[:, u0 : u0 + n, :].rearrange("p t j -> p (t j)"),
                    )
                    u0 += n

        def gather(table, slots, h):
            cols = slice(h * S // 2, (h + 1) * S // 2)
            part = offsets[:, h * S // 32 : (h + 1) * S // 32]
            nc.vector.tensor_copy(slots[:, cols], table[:].indirect(part))

        def gather_words(a, h):
            gather(words[a], slot_words[a], h)

        def gather_scales(i, h):
            gather(scales[i], slot_scales[i], h)

        banks = [psum.tile([P, N], F32, name=f"bank{e}") for e in range(E)]

        def multiply(a, e):
            cols = slice(e * C, (e + 1) * C)
            if a == 0:
                rhs, rhs_scale = w8[:, e, :].bitcast(FP8X4), w8s[:, e, :]
            else:
                rhs, rhs_scale = w4[:, 2 * e + a - 1, :].bitcast(FP4X4), w4s[:, 2 * e + a - 1, :]
            nc.tensor.matmul_mx(
                out=banks[e][:],
                lhsT=slot_words[a][:, cols].bitcast(FP8X4),
                lhsT_scale=slot_scales[planes[a][0]][planes[a][1] : P, cols],
                rhs=rhs,
                rhs_scale=rhs_scale,
                start=(a == 0),
                stop=(a == PASSES - 1),
            )

        def turn(h):
            for half in range(2):
                turned = psum.tile([P, 2, 2 * C], F32, name=f"turned{h}{half}", tag="turned", bufs=4)
                for i in range(2):
                    e = 2 * h + i
                    gated = keep.tile([P, 2 * P], F32, name=f"gated{e}{half}")
                    nc.scalar.activation(gated[:], banks[e][:, half * 2 * P : (half + 1) * 2 * P], COPY, scale=gate_cols[:, e : e + 1])
                    for b in range(2):
                        nc.tensor.transpose(turned[:, b, i * C : (i + 1) * C], gated[:, b * P : (b + 1) * P], ident[:])
                for b in range(2):
                    nc.scalar.copy(slot_y[2 * half + b][:, 2 * h * C : 2 * (h + 1) * C], turned[:, b, :])

        def scatter(b, h):
            part = offsets[:, h * S // 32 : (h + 1) * S // 32]
            nc.vector.tensor_copy(windows[b][:].indirect(part), slot_y[b][:, 2 * h * C : 2 * (h + 1) * C])

        def scatter_all(b):
            nc.vector.tensor_copy(windows[b][:].indirect(offsets[:]), slot_y[b][:])

        def finish(b, engine, parts):
            for i in range(parts):
                cols = slice(i * T // parts, (i + 1) * T // parts)
                engine.tensor_tensor(results[b][:, cols], windows[b][:, cols], residual[:, b, cols], ADD)
                nc.sync.dma_start(out[b * P : (b + 1) * P, cols], results[b][:, cols])

        quantise_pass(0)
        gather_words(0, 0)
        gather_words(0, 1)
        quantise_pass(1)
        gather_words(1, 0)
        gather_scales(0, 0)
        quantise_pass(2)
        gather_words(2, 0)
        gather_scales(1, 0)
        for e in (0, 1):
            for a in range(PASSES):
                multiply(a, e)
        gather_words(1, 1)
        gather_scales(0, 1)
        turn(0)
        gather_words(2, 1)
        gather_scales(1, 1)
        for e in (2, 3):
            for a in range(PASSES):
                multiply(a, e)
        turn(1)

        scatter(0, 0)
        scatter(1, 0)
        scatter(0, 1)
        finish(0, nc.gpsimd, 1)
        scatter(1, 1)
        finish(1, nc.gpsimd, 1)
        scatter_all(2)
        finish(2, nc.gpsimd, 1)
        scatter_all(3)
        finish(3, nc.vector, 2)
